import numpy as np
import ml_dtypes


def mxq(x, axis, fmt="e4m3"):
    dtype, down = {"e4m3": (ml_dtypes.float8_e4m3fn, 7), "e5m2": (ml_dtypes.float8_e5m2, 14)}[fmt]
    v = np.moveaxis(np.asarray(x, np.float32).astype(ml_dtypes.bfloat16).astype(np.float64), axis, -1)
    blocks = v.reshape(v.shape[:-1] + (-1, 32))
    amax = np.abs(blocks).max(-1, keepdims=True)
    byte = np.maximum(np.where(amax > 0, np.frexp(amax)[1] - 1 + 127, 0) - down, 1)
    scale = np.exp2(byte - 127.0)
    codes = (blocks / scale).astype(np.float32).astype(dtype).astype(np.float64)
    return np.moveaxis((codes * scale).reshape(v.shape), -1, axis)


WIDE = False


def mx_kscale(k, group=512):
    if not WIDE:
        return np.ones(k)
    levels = np.array([18, -18])
    if group != 512:
        return np.exp2(np.random.permutation(np.resize(levels, k // group))).repeat(group)
    if k % 512:
        return np.exp2(np.random.permutation(np.resize(levels, k // 32))).repeat(32)
    a = np.empty((k // 512, 16))
    for p in range(k // 512):
        a[p, :8] = np.random.permutation(np.resize(levels, 8))
        for g in range(8):
            far = levels[np.abs(levels - a[p, g]) >= 10]
            a[p, g + 8] = far[np.random.randint(len(far))]
    return np.exp2(a.ravel()).repeat(32)


def f64(x):
    return np.asarray(x).astype(np.float64)


G, D, M, O, N = 4, 128, 128, 128, 512


def sgn(shape):
    return np.random.uniform(0.5, 2.0, shape) * np.where(np.random.standard_normal(shape) < 0, -1.0, 1.0)


def setup_inputs():
    n = np.random.standard_normal
    s_d = mx_kscale(D, 0)
    s_m = mx_kscale(M, 0)
    return {
        "x": (n((G, D, N)) * s_d[:, None]).astype(np.float32),
        "w1": (n((G, D, M)) / np.sqrt(D) / s_d[:, None]).astype(np.float32),
        "w2": (n((G, D, M)) / np.sqrt(D) / s_d[:, None]).astype(np.float32),
        "tp": (np.random.uniform(0.5, 1.2, (G, M, 1))).astype(np.float32),
        "hs": (sgn((G, M, 1)) * s_m[:, None]).astype(np.float32),
        "wo2": (n((G, M, O)) / np.sqrt(M) / s_m[:, None]).astype(np.float32),
        "res": (0.5 * n((G, O, N))).astype(np.float32),
    }


def reference(x, w1, w2, tp, hs, wo2, res):
    w1q = mxq(f64(w1), 1, "e4m3")
    xq = mxq(f64(x), 1, "e4m3")
    z1 = w1q.transpose(0, 2, 1) @ xq
    w2q = mxq(f64(w2), 1, "e4m3")
    z2 = w2q.transpose(0, 2, 1) @ xq
    p1 = np.exp(z1 * f64(tp) - np.max(z1 * f64(tp), axis=-1, keepdims=True))
    zs = np.sum(p1, axis=-1, keepdims=True)
    h = p1 / zs * z2 * 512.0
    hh = h * f64(hs)
    wo2q = mxq(f64(wo2), 1, "e4m3")
    hhq = mxq(hh, 1, "e4m3")
    y0 = wo2q.transpose(0, 2, 1) @ hhq
    y = y0 + f64(res)
    return y

@@ -1,0 +1,213 @@
+from contextlib import ExitStack
+
+import concourse.mybir as mybir
+
+G, D, M, O, N = 4, 128, 128, 128, 512
+FLOPS = 2 * G * N * (2 * D * M + M * O)
+
+F32 = mybir.dt.float32
+BF16 = mybir.dt.bfloat16
+U32 = mybir.dt.uint32
+U8 = mybir.dt.uint8
+FP8X4 = mybir.dt.float8_e4m3fn_x4
+ALU = mybir.AluOpType
+ACT = mybir.ActivationFunctionType
+
+P = 128
+PACK = 4
+R = 32
+NB = 128
+HALF = N // 2
+RUN = 4
+HH_SPLIT = 176
+
+
+def word_views(words, rows):
+    return (
+        words.rearrange("p (c i) j -> p c j i", i=RUN),
+        rows.rearrange("p j (c i) -> p c j i", i=RUN),
+    )
+
+
+def tile_rows_frowsoft_kernel(tc, x, w1, w2, tp, hs, wo2, res, out):
+    nc = tc.nc
+
+    with ExitStack() as ctx:
+        sb = ctx.enter_context(tc.tile_pool(name="sb", bufs=1))
+        ps = ctx.enter_context(tc.psum_pool(name="ps", bufs=1))
+        ctx.enter_context(tc.manual_schedule())
+
+        def packed_rows(dram):
+            return dram.rearrange("g (p j) n -> (g p) j n", j=PACK)
+
+        def operand(name, width):
+            words = sb.tile([P, width, PACK], BF16, name=name + "_words", align_bytes=64)
+            codes = sb.tile([P, width], U32, name=name + "_codes", align_bytes=64)
+            scales = sb.tile([P, width], U8, name=name + "_scales", align_bytes=64)
+            return words, codes, scales
+
+        def interleave_vector(words, rows):
+            dst, src = word_views(words, rows)
+            nc.vector.tensor_copy(out=dst, in_=src)
+
+        def interleave_scalar(words, rows):
+            dst, src = word_views(words, rows)
+            nc.scalar.activation(out=dst, in_=src, func=ACT.Copy)
+
+        def quantize(op):
+            words, codes, scales = op
+            nc.vector.quantize_mx(
+                out=codes[:].bitcast(FP8X4),
+                scales=scales[:],
+                in_=words[:].rearrange("p n j -> p (n j)"),
+            )
+
+        def product(dst, g, weights, moving):
+            rows = slice(R * g, R * (g + 1))
+            for c0 in range(0, HALF, NB):
+                cols = slice(c0, c0 + NB)
+                nc.tensor.matmul_mx(
+                    out=dst[:, cols],
+                    lhsT=weights[1][rows, :].bitcast(FP8X4),
+                    lhsT_scale=weights[2][rows, :],
+                    rhs=moving[1][rows, cols].bitcast(FP8X4),
+                    rhs_scale=moving[2][rows, cols],
+                    start=True,
+                    stop=True,
+                )
+
+        halves = [slice(0, HALF), slice(HALF, N)]
+
+        x_rows = sb.tile([P, PACK, N], F32)
+        w1_rows = sb.tile([P, PACK, M], F32)
+        w2_rows = sb.tile([P, PACK, M], F32)
+        wo_rows = sb.tile([P, PACK, O], F32)
+        res_sb = sb.tile([P, G, N], F32)
+        tp_sb = sb.tile([P, G], F32)
+        hs_sb = sb.tile([P, G], F32)
+
+        nc.sync.dma_start(out=x_rows[:], in_=packed_rows(x))
+        nc.sync.dma_start(out=w1_rows[:], in_=packed_rows(w1))
+        with nc.allow_non_contiguous_dma(reason="one float32 for each feature and group"):
+            nc.sync.dma_start(out=tp_sb[:], in_=tp.rearrange("g m o -> m (g o)"))
+        nc.sync.dma_start(out=w2_rows[:], in_=packed_rows(w2))
+        with nc.allow_non_contiguous_dma(reason="one float32 for each feature and group"):
+            nc.sync.dma_start(out=hs_sb[:], in_=hs.rearrange("g m o -> m (g o)"))
+        nc.sync.dma_start(out=wo_rows[:], in_=packed_rows(wo2))
+        nc.sync.dma_start(out=res_sb[:], in_=res.rearrange("g o n -> o g n"))
+
+        xq = [operand("x%d" % h, HALF) for h in range(2)]
+        w1q = operand("w1", M)
+        w2q = operand("w2", M)
+        woq = operand("wo", O)
+
+        interleave_vector(xq[0][0][:], x_rows[:, :, halves[0]])
+        interleave_scalar(xq[1][0][:], x_rows[:, :, halves[1]])
+        interleave_vector(w1q[0][:], w1_rows[:])
+        quantize(xq[0])
+        quantize(w1q)
+        quantize(xq[1])
+
+        neg_tp = sb.tile([P, G], F32)
+        nc.scalar.activation(out=neg_tp[:], in_=tp_sb[:], func=ACT.Copy, scale=-1.0)
+        interleave_scalar(w2q[0][:], w2_rows[:])
+        quantize(w2q)
+
+        bank1 = [ps.tile([P, N], F32, name="bank1_%d" % g) for g in range(G)]
+        bank2 = [ps.tile([P, N], F32, name="bank2_%d" % g) for g in range(G)]
+
+        for pair in ((0, 1), (2,), (3,)):
+            for h in range(2):
+                for g in pair:
+                    product(bank1[g][:, halves[h]], g, w1q, xq[h])
+        for g in range(G):
+            for h in range(2):
+                product(bank2[g][:, halves[h]], g, w2q, xq[h])
+
+        neg_max = sb.tile([P, G], F32)
+        zs = sb.tile([P, G], F32)
+        inv = sb.tile([P, G], F32)
+        factor = sb.tile([P, G], F32)
+        neg_t = [sb.tile([P, N], F32, name="neg_t%d" % g) for g in range(G)]
+        p1 = [sb.tile([P, N], F32, name="p1_%d" % g) for g in range(G)]
+        hh = [[sb.tile([P, HALF], BF16, name="hh%d_%d" % (h, g)) for g in range(G)] for h in range(2)]
+        hh_rows = [sb.tile([P, PACK, HALF], BF16, name="hh_rows%d" % h) for h in range(2)]
+        hq = [operand("hh%d" % h, HALF) for h in range(2)]
+
+        def softmax_numerators(g):
+            col = slice(g, g + 1)
+            nc.vector.tensor_scalar(
+                out=neg_t[g][:], in0=bank1[g][:], scalar1=neg_tp[:, col], scalar2=None,
+                op0=ALU.mult, op1=ALU.min, accum_out=neg_max[:, col],
+            )
+            nc.scalar.activation(
+                out=p1[g][:], in_=neg_t[g][:], func=ACT.Exp,
+                bias=neg_max[:, col], scale=-1.0, accum_out=zs[:, col],
+            )
+
+        def invert(cols):
+            nc.vector.reciprocal(out=inv[:, cols], in_=zs[:, cols])
+
+        def row_factor(cols):
+            nc.vector.scalar_tensor_tensor(
+                out=factor[:, cols], in0=inv[:, cols], scalar=float(N), in1=hs_sb[:, cols],
+                op0=ALU.mult, op1=ALU.mult,
+            )
+
+        def make_hh(h, g):
+            nc.vector.scalar_tensor_tensor(
+                out=hh[h][g][:], in0=p1[g][:, halves[h]], scalar=factor[:, g : g + 1],
+                in1=bank2[g][:, halves[h]], op0=ALU.mult, op1=ALU.mult,
+            )
+            nc.sync.dma_start(out=hh_rows[h][R * g : R * (g + 1), :, :], in_=hh[h][g][:])
+
+        softmax_numerators(0)
+        softmax_numerators(1)
+        softmax_numerators(2)
+        invert(slice(0, 1))
+        softmax_numerators(3)
+        row_factor(slice(0, 1))
+        invert(slice(1, 3))
+        make_hh(0, 0)
+        row_factor(slice(1, 3))
+        make_hh(0, 1)
+        invert(slice(3, 4))
+        make_hh(0, 2)
+        row_factor(slice(3, 4))
+        make_hh(1, 0)
+        make_hh(0, 3)
+        for g in range(1, G):
+            make_hh(1, g)
+
+        interleave_scalar(woq[0][:], wo_rows[:])
+        quantize(woq)
+
+        y_bank = [bank1, bank2]
+        y = [[sb.tile([P, HALF], F32, name="y%d_%d" % (h, g)) for g in range(G)] for h in range(2)]
+
+        def interleave_hh(h):
+            interleave_vector(hq[h][0][:, :HH_SPLIT, :], hh_rows[h][:, :, :HH_SPLIT])
+            dst, src = word_views(hq[h][0][:, HH_SPLIT:, :], hh_rows[h][:, :, HH_SPLIT:])
+            nc.scalar.copy(out=dst, in_=src)
+
+        def second_products(h):
+            for g in range(G):
+                product(y_bank[h][g][:, :HALF], g, woq, hq[h])
+
+        def finish(h, g):
+            nc.vector.tensor_tensor(
+                out=y[h][g][:], in0=y_bank[h][g][:, :HALF], in1=res_sb[:, g, halves[h]], op=ALU.add,
+            )
+            nc.sync.dma_start(out=out[g, :, halves[h]], in_=y[h][g][:])
+
+        interleave_hh(0)
+        quantize(hq[0])
+        second_products(0)
+        interleave_hh(1)
+        finish(0, 0)
+        quantize(hq[1])
+        second_products(1)
+        for g in range(1, G):
+            finish(0, g)
+        for g in range(G):
+            finish(1, g)

@@ -19,7 +19,9 @@ R = 32
 NB = 128
 HALF = N // 2
 RUN = 4
-HH_SPLIT = 176
+CHUNKS = ((0, 256, 176), (256, 512, 128))
+STEP = R // G
+HS_ROW = STEP // 2
 
 
 def word_views(words, rows):
@@ -64,7 +66,7 @@ def tile_rows_frowsoft_kernel(tc, x, w1, w2, tp, hs, wo2, res, out):
 
         def product(dst, g, weights, moving):
             rows = slice(R * g, R * (g + 1))
-            for c0 in range(0, HALF, NB):
+            for c0 in range(0, dst.shape[1], NB):
                 cols = slice(c0, c0 + NB)
                 nc.tensor.matmul_mx(
                     out=dst[:, cols],
@@ -83,16 +85,18 @@ def tile_rows_frowsoft_kernel(tc, x, w1, w2, tp, hs, wo2, res, out):
         w2_rows = sb.tile([P, PACK, M], F32)
         wo_rows = sb.tile([P, PACK, O], F32)
         res_sb = sb.tile([P, G, N], F32)
-        tp_sb = sb.tile([P, G], F32)
-        hs_sb = sb.tile([P, G], F32)
+        vec_rows = sb.tile([P, R], F32, align_bytes=64)
+        vec_cols = sb.tile([P, R], F32, align_bytes=64)
 
+        def quadrant_rows(vec):
+            return vec.rearrange("g (q c) o -> q g (c o)", c=R)
+
+        nc.vector.memset(vec_rows[:], 0.0)
         nc.sync.dma_start(out=x_rows[:], in_=packed_rows(x))
         nc.sync.dma_start(out=w1_rows[:], in_=packed_rows(w1))
-        with nc.allow_non_contiguous_dma(reason="one float32 for each feature and group"):
-            nc.sync.dma_start(out=tp_sb[:], in_=tp.rearrange("g m o -> m (g o)"))
         nc.sync.dma_start(out=w2_rows[:], in_=packed_rows(w2))
-        with nc.allow_non_contiguous_dma(reason="one float32 for each feature and group"):
-            nc.sync.dma_start(out=hs_sb[:], in_=hs.rearrange("g m o -> m (g o)"))
+        nc.sync.dma_start(out=vec_rows[0:P:STEP, :], in_=quadrant_rows(tp))
+        nc.sync.dma_start(out=vec_rows[HS_ROW:P:STEP, :], in_=quadrant_rows(hs))
         nc.sync.dma_start(out=wo_rows[:], in_=packed_rows(wo2))
         nc.sync.dma_start(out=res_sb[:], in_=res.rearrange("g o n -> o g n"))
 
@@ -107,11 +111,14 @@ def tile_rows_frowsoft_kernel(tc, x, w1, w2, tp, hs, wo2, res, out):
         quantize(xq[0])
         quantize(w1q)
         quantize(xq[1])
-
-        neg_tp = sb.tile([P, G], F32)
-        nc.scalar.activation(out=neg_tp[:], in_=tp_sb[:], func=ACT.Copy, scale=-1.0)
+        nc.vector.transpose(out=vec_cols[:], in_=vec_rows[:])
         interleave_scalar(w2q[0][:], w2_rows[:])
         quantize(w2q)
+        hs_sb = vec_cols[:, HS_ROW:R:STEP]
+        neg_tp = sb.tile([P, G], F32)
+        nc.vector.tensor_scalar(
+            out=neg_tp[:], in0=vec_cols[:, 0:R:STEP], scalar1=-1.0, scalar2=None, op0=ALU.mult,
+        )
 
         bank1 = [ps.tile([P, N], F32, name="bank1_%d" % g) for g in range(G)]
         bank2 = [ps.tile([P, N], F32, name="bank2_%d" % g) for g in range(G)]
@@ -120,9 +127,6 @@ def tile_rows_frowsoft_kernel(tc, x, w1, w2, tp, hs, wo2, res, out):
             for h in range(2):
                 for g in pair:
                     product(bank1[g][:, halves[h]], g, w1q, xq[h])
-        for g in range(G):
-            for h in range(2):
-                product(bank2[g][:, halves[h]], g, w2q, xq[h])
 
         neg_max = sb.tile([P, G], F32)
         zs = sb.tile([P, G], F32)
@@ -130,9 +134,14 @@ def tile_rows_frowsoft_kernel(tc, x, w1, w2, tp, hs, wo2, res, out):
         factor = sb.tile([P, G], F32)
         neg_t = [sb.tile([P, N], F32, name="neg_t%d" % g) for g in range(G)]
         p1 = [sb.tile([P, N], F32, name="p1_%d" % g) for g in range(G)]
-        hh = [[sb.tile([P, HALF], BF16, name="hh%d_%d" % (h, g)) for g in range(G)] for h in range(2)]
-        hh_rows = [sb.tile([P, PACK, HALF], BF16, name="hh_rows%d" % h) for h in range(2)]
-        hq = [operand("hh%d" % h, HALF) for h in range(2)]
+        cols_of = [slice(a, b) for a, b, split in CHUNKS]
+        width = [b - a for a, b, split in CHUNKS]
+        hh = [
+            [sb.tile([P, width[k]], BF16, name="hh%d_%d" % (k, g)) for g in range(G)]
+            for k in range(len(CHUNKS))
+        ]
+        hh_rows = [sb.tile([P, PACK, width[k]], BF16, name="hh_rows%d" % k) for k in range(len(CHUNKS))]
+        hq = [operand("hh%d" % k, width[k]) for k in range(len(CHUNKS))]
 
         def softmax_numerators(g):
             col = slice(g, g + 1)
@@ -154,51 +163,51 @@ def tile_rows_frowsoft_kernel(tc, x, w1, w2, tp, hs, wo2, res, out):
                 op0=ALU.mult, op1=ALU.mult,
             )
 
-        def make_hh(h, g):
+        def make_hh(k, g):
             nc.vector.scalar_tensor_tensor(
-                out=hh[h][g][:], in0=p1[g][:, halves[h]], scalar=factor[:, g : g + 1],
-                in1=bank2[g][:, halves[h]], op0=ALU.mult, op1=ALU.mult,
+                out=hh[k][g][:], in0=p1[g][:, cols_of[k]], scalar=factor[:, g : g + 1],
+                in1=bank2[g][:, cols_of[k]], op0=ALU.mult, op1=ALU.mult,
             )
-            nc.sync.dma_start(out=hh_rows[h][R * g : R * (g + 1), :, :], in_=hh[h][g][:])
+            nc.sync.dma_start(out=hh_rows[k][R * g : R * (g + 1), :, :], in_=hh[k][g][:])
 
-        softmax_numerators(0)
-        softmax_numerators(1)
-        softmax_numerators(2)
-        invert(slice(0, 1))
-        softmax_numerators(3)
-        row_factor(slice(0, 1))
-        invert(slice(1, 3))
+        for g in range(G):
+            for h in range(2):
+                product(bank2[g][:, halves[h]], g, w2q, xq[h])
+        for g in range(G):
+            softmax_numerators(g)
+        invert(slice(0, 3))
+        row_factor(slice(0, 3))
         make_hh(0, 0)
-        row_factor(slice(1, 3))
-        make_hh(0, 1)
         invert(slice(3, 4))
-        make_hh(0, 2)
+        make_hh(0, 1)
         row_factor(slice(3, 4))
-        make_hh(1, 0)
+        make_hh(0, 2)
         make_hh(0, 3)
-        for g in range(1, G):
+        for g in range(G):
             make_hh(1, g)
 
         interleave_scalar(woq[0][:], wo_rows[:])
         quantize(woq)
 
         y_bank = [bank1, bank2]
-        y = [[sb.tile([P, HALF], F32, name="y%d_%d" % (h, g)) for g in range(G)] for h in range(2)]
+        y = [sb.tile([P, G, width[k]], F32, name="y%d" % k) for k in range(len(CHUNKS))]
 
-        def interleave_hh(h):
-            interleave_vector(hq[h][0][:, :HH_SPLIT, :], hh_rows[h][:, :, :HH_SPLIT])
-            dst, src = word_views(hq[h][0][:, HH_SPLIT:, :], hh_rows[h][:, :, HH_SPLIT:])
+        def interleave_hh(k):
+            split = CHUNKS[k][2]
+            if split:
+                interleave_vector(hq[k][0][:, :split, :], hh_rows[k][:, :, :split])
+            dst, src = word_views(hq[k][0][:, split:, :], hh_rows[k][:, :, split:])
             nc.scalar.copy(out=dst, in_=src)
 
-        def second_products(h):
+        def second_products(k):
             for g in range(G):
-                product(y_bank[h][g][:, :HALF], g, woq, hq[h])
+                product(y_bank[k][g][:, cols_of[k]], g, woq, hq[k])
 
-        def finish(h, g):
+        def finish(k, g):
             nc.vector.tensor_tensor(
-                out=y[h][g][:], in0=y_bank[h][g][:, :HALF], in1=res_sb[:, g, halves[h]], op=ALU.add,
+                out=y[k][:, g, :], in0=y_bank[k][g][:, cols_of[k]], in1=res_sb[:, g, cols_of[k]], op=ALU.add,
             )
-            nc.sync.dma_start(out=out[g, :, halves[h]], in_=y[h][g][:])
+            nc.sync.dma_start(out=out[g, :, cols_of[k]], in_=y[k][:, g, :])
 
         interleave_hh(0)
         quantize(hq[0])

@@ -19,9 +19,9 @@ R = 32
 NB = 128
 HALF = N // 2
 RUN = 4
-CHUNKS = ((0, 256, 176), (256, 512, 128))
 STEP = R // G
 HS_ROW = STEP // 2
+PIECES = ((0, 0, 256, 176), (1, 0, 256, 176))
 
 
 def word_views(words, rows):
@@ -79,6 +79,7 @@ def tile_rows_frowsoft_kernel(tc, x, w1, w2, tp, hs, wo2, res, out):
                 )
 
         halves = [slice(0, HALF), slice(HALF, N)]
+        col = [slice(g, g + 1) for g in range(G)]
 
         x_rows = sb.tile([P, PACK, N], F32)
         w1_rows = sb.tile([P, PACK, M], F32)
@@ -113,20 +114,24 @@ def tile_rows_frowsoft_kernel(tc, x, w1, w2, tp, hs, wo2, res, out):
         quantize(xq[1])
         nc.vector.transpose(out=vec_cols[:], in_=vec_rows[:])
         interleave_scalar(w2q[0][:], w2_rows[:])
+        interleave_scalar(woq[0][:], wo_rows[:])
         quantize(w2q)
-        hs_sb = vec_cols[:, HS_ROW:R:STEP]
         neg_tp = sb.tile([P, G], F32)
+        gain = sb.tile([P, G], F32)
         nc.vector.tensor_scalar(
             out=neg_tp[:], in0=vec_cols[:, 0:R:STEP], scalar1=-1.0, scalar2=None, op0=ALU.mult,
+        )
+        nc.vector.tensor_scalar(
+            out=gain[:], in0=vec_cols[:, HS_ROW:R:STEP], scalar1=float(N), scalar2=None, op0=ALU.mult,
         )
 
         bank1 = [ps.tile([P, N], F32, name="bank1_%d" % g) for g in range(G)]
         bank2 = [ps.tile([P, N], F32, name="bank2_%d" % g) for g in range(G)]
 
-        for pair in ((0, 1), (2,), (3,)):
-            for h in range(2):
-                for g in pair:
-                    product(bank1[g][:, halves[h]], g, w1q, xq[h])
+        for bank, weights in ((bank1, w1q), (bank2, w2q)):
+            for g in range(G):
+                for h in range(2):
+                    product(bank[g][:, halves[h]], g, weights, xq[h])
 
         neg_max = sb.tile([P, G], F32)
         zs = sb.tile([P, G], F32)
@@ -134,89 +139,96 @@ def tile_rows_frowsoft_kernel(tc, x, w1, w2, tp, hs, wo2, res, out):
         factor = sb.tile([P, G], F32)
         neg_t = [sb.tile([P, N], F32, name="neg_t%d" % g) for g in range(G)]
         p1 = [sb.tile([P, N], F32, name="p1_%d" % g) for g in range(G)]
-        cols_of = [slice(a, b) for a, b, split in CHUNKS]
-        width = [b - a for a, b, split in CHUNKS]
-        hh = [
-            [sb.tile([P, width[k]], BF16, name="hh%d_%d" % (k, g)) for g in range(G)]
-            for k in range(len(CHUNKS))
-        ]
-        hh_rows = [sb.tile([P, PACK, width[k]], BF16, name="hh_rows%d" % k) for k in range(len(CHUNKS))]
-        hq = [operand("hh%d" % k, width[k]) for k in range(len(CHUNKS))]
+        raw = [sb.tile([P, HALF], F32, name="raw%d" % g) for g in range(G)]
+        hh = [[sb.tile([P, HALF], BF16, name="hh%d_%d" % (h, g)) for g in range(G)] for h in range(2)]
+        hh_rows = [sb.tile([P, PACK, HALF], BF16, name="hh_rows%d" % h) for h in range(2)]
 
         def softmax_numerators(g):
-            col = slice(g, g + 1)
             nc.vector.tensor_scalar(
-                out=neg_t[g][:], in0=bank1[g][:], scalar1=neg_tp[:, col], scalar2=None,
-                op0=ALU.mult, op1=ALU.min, accum_out=neg_max[:, col],
+                out=neg_t[g][:], in0=bank1[g][:], scalar1=neg_tp[:, col[g]], scalar2=None,
+                op0=ALU.mult, op1=ALU.min, accum_out=neg_max[:, col[g]],
             )
             nc.scalar.activation(
                 out=p1[g][:], in_=neg_t[g][:], func=ACT.Exp,
-                bias=neg_max[:, col], scale=-1.0, accum_out=zs[:, col],
+                bias=neg_max[:, col[g]], scale=-1.0, accum_out=zs[:, col[g]],
             )
 
         def invert(cols):
             nc.vector.reciprocal(out=inv[:, cols], in_=zs[:, cols])
 
+        def weigh(dst, h, g, scalar):
+            nc.vector.scalar_tensor_tensor(
+                out=dst[:], in0=p1[g][:, halves[h]], scalar=scalar[:, col[g]],
+                in1=bank2[g][:, halves[h]], op0=ALU.mult, op1=ALU.mult,
+            )
+
+        def normalise_scalar(g):
+            nc.scalar.activation(out=hh[0][g][:], in_=raw[g][:], func=ACT.Copy, scale=inv[:, col[g]])
+
+        def normalise_vector(g):
+            nc.vector.tensor_scalar(
+                out=hh[0][g][:], in0=raw[g][:], scalar1=inv[:, col[g]], scalar2=None, op0=ALU.mult,
+            )
+
         def row_factor(cols):
-            nc.vector.scalar_tensor_tensor(
-                out=factor[:, cols], in0=inv[:, cols], scalar=float(N), in1=hs_sb[:, cols],
-                op0=ALU.mult, op1=ALU.mult,
-            )
+            nc.vector.tensor_tensor(out=factor[:, cols], in0=inv[:, cols], in1=gain[:, cols], op=ALU.mult)
 
-        def make_hh(k, g):
-            nc.vector.scalar_tensor_tensor(
-                out=hh[k][g][:], in0=p1[g][:, cols_of[k]], scalar=factor[:, g : g + 1],
-                in1=bank2[g][:, cols_of[k]], op0=ALU.mult, op1=ALU.mult,
-            )
-            nc.sync.dma_start(out=hh_rows[k][R * g : R * (g + 1), :, :], in_=hh[k][g][:])
+        def send_hh(h, g):
+            nc.sync.dma_start(out=hh_rows[h][R * g : R * (g + 1), :, :], in_=hh[h][g][:])
 
-        for g in range(G):
-            for h in range(2):
-                product(bank2[g][:, halves[h]], g, w2q, xq[h])
         for g in range(G):
             softmax_numerators(g)
+        weigh(raw[0], 0, 0, gain)
+        weigh(raw[1], 0, 1, gain)
         invert(slice(0, 3))
-        row_factor(slice(0, 3))
-        make_hh(0, 0)
-        invert(slice(3, 4))
-        make_hh(0, 1)
-        row_factor(slice(3, 4))
-        make_hh(0, 2)
-        make_hh(0, 3)
+        weigh(raw[2], 0, 2, gain)
+        invert(col[3])
+        weigh(raw[3], 0, 3, gain)
+        normalise_scalar(0)
+        normalise_scalar(1)
+        normalise_vector(2)
+        row_factor(slice(0, 4))
+        normalise_vector(3)
         for g in range(G):
-            make_hh(1, g)
-
-        interleave_scalar(woq[0][:], wo_rows[:])
+            weigh(hh[1][g], 1, g, factor)
+        for h in range(2):
+            for g in range(G):
+                send_hh(h, g)
         quantize(woq)
 
         y_bank = [bank1, bank2]
-        y = [sb.tile([P, G, width[k]], F32, name="y%d" % k) for k in range(len(CHUNKS))]
+        width = [b - a for h, a, b, split in PIECES]
+        hq = [operand("hh%d" % k, width[k]) for k in range(len(PIECES))]
+        y = [sb.tile([P, G, width[k]], F32, name="y%d" % k) for k in range(len(PIECES))]
+        out_v = out.rearrange("g o n -> o g n")
 
         def interleave_hh(k):
-            split = CHUNKS[k][2]
-            if split:
-                interleave_vector(hq[k][0][:, :split, :], hh_rows[k][:, :, :split])
-            dst, src = word_views(hq[k][0][:, split:, :], hh_rows[k][:, :, split:])
+            h, a, b, split = PIECES[k]
+            interleave_vector(hq[k][0][:, :split, :], hh_rows[h][:, :, a : a + split])
+            dst, src = word_views(hq[k][0][:, split:, :], hh_rows[h][:, :, a + split : b])
             nc.scalar.copy(out=dst, in_=src)
 
         def second_products(k):
+            h, a, b, split = PIECES[k]
+            quantize(hq[k])
             for g in range(G):
-                product(y_bank[k][g][:, cols_of[k]], g, woq, hq[k])
+                product(y_bank[h][g][:, a:b], g, woq, hq[k])
 
-        def finish(k, g):
-            nc.vector.tensor_tensor(
-                out=y[k][:, g, :], in0=y_bank[k][g][:, cols_of[k]], in1=res_sb[:, g, cols_of[k]], op=ALU.add,
-            )
-            nc.sync.dma_start(out=out[g, :, cols_of[k]], in_=y[k][:, g, :])
+        def finish(k, groups):
+            h, a, b, split = PIECES[k]
+            cols = slice(HALF * h + a, HALF * h + b)
+            for g in range(groups.start, groups.stop):
+                nc.vector.tensor_tensor(
+                    out=y[k][:, g, :], in0=y_bank[h][g][:, a:b], in1=res_sb[:, g, cols], op=ALU.add,
+                )
+            nc.sync.dma_start(out=out_v[:, groups, cols], in_=y[k][:, groups, :])
 
         interleave_hh(0)
-        quantize(hq[0])
         second_products(0)
         interleave_hh(1)
-        finish(0, 0)
-        quantize(hq[1])
+        finish(0, col[0])
         second_products(1)
         for g in range(1, G):
-            finish(0, g)
+            finish(0, col[g])
         for g in range(G):
-            finish(1, g)
+            finish(1, col[g])

from contextlib import ExitStack

import concourse.mybir as mybir

G, D, M, O, N = 4, 128, 128, 128, 512
FLOPS = 2 * G * N * (2 * D * M + M * O)

F32 = mybir.dt.float32
BF16 = mybir.dt.bfloat16
U32 = mybir.dt.uint32
U8 = mybir.dt.uint8
FP8X4 = mybir.dt.float8_e4m3fn_x4
ALU = mybir.AluOpType
ACT = mybir.ActivationFunctionType

P = 128
PACK = 4
R = 32
NB = 128
HALF = N // 2
RUN = 4
STEP = R // G
HS_ROW = STEP // 2
PIECES = ((0, 0, 256, 176), (1, 0, 256, 176))


def word_views(words, rows):
    return (
        words.rearrange("p (c i) j -> p c j i", i=RUN),
        rows.rearrange("p j (c i) -> p c j i", i=RUN),
    )


def tile_rows_frowsoft_kernel(tc, x, w1, w2, tp, hs, wo2, res, out):
    nc = tc.nc

    with ExitStack() as ctx:
        sb = ctx.enter_context(tc.tile_pool(name="sb", bufs=1))
        ps = ctx.enter_context(tc.psum_pool(name="ps", bufs=1))
        ctx.enter_context(tc.manual_schedule())

        def packed_rows(dram):
            return dram.rearrange("g (p j) n -> (g p) j n", j=PACK)

        def operand(name, width):
            words = sb.tile([P, width, PACK], BF16, name=name + "_words", align_bytes=64)
            codes = sb.tile([P, width], U32, name=name + "_codes", align_bytes=64)
            scales = sb.tile([P, width], U8, name=name + "_scales", align_bytes=64)
            return words, codes, scales

        def interleave_vector(words, rows):
            dst, src = word_views(words, rows)
            nc.vector.tensor_copy(out=dst, in_=src)

        def interleave_scalar(words, rows):
            dst, src = word_views(words, rows)
            nc.scalar.activation(out=dst, in_=src, func=ACT.Copy)

        def quantize(op):
            words, codes, scales = op
            nc.vector.quantize_mx(
                out=codes[:].bitcast(FP8X4),
                scales=scales[:],
                in_=words[:].rearrange("p n j -> p (n j)"),
            )

        def product(dst, g, weights, moving):
            rows = slice(R * g, R * (g + 1))
            for c0 in range(0, dst.shape[1], NB):
                cols = slice(c0, c0 + NB)
                nc.tensor.matmul_mx(
                    out=dst[:, cols],
                    lhsT=weights[1][rows, :].bitcast(FP8X4),
                    lhsT_scale=weights[2][rows, :],
                    rhs=moving[1][rows, cols].bitcast(FP8X4),
                    rhs_scale=moving[2][rows, cols],
                    start=True,
                    stop=True,
                )

        halves = [slice(0, HALF), slice(HALF, N)]
        col = [slice(g, g + 1) for g in range(G)]

        x_rows = sb.tile([P, PACK, N], F32)
        w1_rows = sb.tile([P, PACK, M], F32)
        w2_rows = sb.tile([P, PACK, M], F32)
        wo_rows = sb.tile([P, PACK, O], F32)
        res_sb = sb.tile([P, G, N], F32)
        vec_rows = sb.tile([P, R], F32, align_bytes=64)
        vec_cols = sb.tile([P, R], F32, align_bytes=64)

        def quadrant_rows(vec):
            return vec.rearrange("g (q c) o -> q g (c o)", c=R)

        nc.vector.memset(vec_rows[:], 0.0)
        nc.sync.dma_start(out=x_rows[:], in_=packed_rows(x))
        nc.sync.dma_start(out=w1_rows[:], in_=packed_rows(w1))
        nc.sync.dma_start(out=w2_rows[:], in_=packed_rows(w2))
        nc.sync.dma_start(out=vec_rows[0:P:STEP, :], in_=quadrant_rows(tp))
        nc.sync.dma_start(out=vec_rows[HS_ROW:P:STEP, :], in_=quadrant_rows(hs))
        nc.sync.dma_start(out=wo_rows[:], in_=packed_rows(wo2))
        nc.sync.dma_start(out=res_sb[:], in_=res.rearrange("g o n -> o g n"))

        xq = [operand("x%d" % h, HALF) for h in range(2)]
        w1q = operand("w1", M)
        w2q = operand("w2", M)
        woq = operand("wo", O)

        interleave_vector(xq[0][0][:], x_rows[:, :, halves[0]])
        interleave_scalar(xq[1][0][:], x_rows[:, :, halves[1]])
        interleave_vector(w1q[0][:], w1_rows[:])
        quantize(xq[0])
        quantize(w1q)
        quantize(xq[1])
        nc.vector.transpose(out=vec_cols[:], in_=vec_rows[:])
        interleave_scalar(w2q[0][:], w2_rows[:])
        interleave_scalar(woq[0][:], wo_rows[:])
        quantize(w2q)
        neg_tp = sb.tile([P, G], F32)
        gain = sb.tile([P, G], F32)
        nc.vector.tensor_scalar(
            out=neg_tp[:], in0=vec_cols[:, 0:R:STEP], scalar1=-1.0, scalar2=None, op0=ALU.mult,
        )
        nc.vector.tensor_scalar(
            out=gain[:], in0=vec_cols[:, HS_ROW:R:STEP], scalar1=float(N), scalar2=None, op0=ALU.mult,
        )

        bank1 = [ps.tile([P, N], F32, name="bank1_%d" % g) for g in range(G)]
        bank2 = [ps.tile([P, N], F32, name="bank2_%d" % g) for g in range(G)]

        for bank, weights in ((bank1, w1q), (bank2, w2q)):
            for g in range(G):
                for h in range(2):
                    product(bank[g][:, halves[h]], g, weights, xq[h])

        neg_max = sb.tile([P, G], F32)
        zs = sb.tile([P, G], F32)
        inv = sb.tile([P, G], F32)
        factor = sb.tile([P, G], F32)
        neg_t = [sb.tile([P, N], F32, name="neg_t%d" % g) for g in range(G)]
        p1 = [sb.tile([P, N], F32, name="p1_%d" % g) for g in range(G)]
        raw = [sb.tile([P, HALF], F32, name="raw%d" % g) for g in range(G)]
        hh = [[sb.tile([P, HALF], BF16, name="hh%d_%d" % (h, g)) for g in range(G)] for h in range(2)]
        hh_rows = [sb.tile([P, PACK, HALF], BF16, name="hh_rows%d" % h) for h in range(2)]

        def softmax_numerators(g):
            nc.vector.tensor_scalar(
                out=neg_t[g][:], in0=bank1[g][:], scalar1=neg_tp[:, col[g]], scalar2=None,
                op0=ALU.mult, op1=ALU.min, accum_out=neg_max[:, col[g]],
            )
            nc.scalar.activation(
                out=p1[g][:], in_=neg_t[g][:], func=ACT.Exp,
                bias=neg_max[:, col[g]], scale=-1.0, accum_out=zs[:, col[g]],
            )

        def invert(cols):
            nc.vector.reciprocal(out=inv[:, cols], in_=zs[:, cols])

        def weigh(dst, h, g, scalar):
            nc.vector.scalar_tensor_tensor(
                out=dst[:], in0=p1[g][:, halves[h]], scalar=scalar[:, col[g]],
                in1=bank2[g][:, halves[h]], op0=ALU.mult, op1=ALU.mult,
            )

        def normalise_scalar(g):
            nc.scalar.activation(out=hh[0][g][:], in_=raw[g][:], func=ACT.Copy, scale=inv[:, col[g]])

        def normalise_vector(g):
            nc.vector.tensor_scalar(
                out=hh[0][g][:], in0=raw[g][:], scalar1=inv[:, col[g]], scalar2=None, op0=ALU.mult,
            )

        def row_factor(cols):
            nc.vector.tensor_tensor(out=factor[:, cols], in0=inv[:, cols], in1=gain[:, cols], op=ALU.mult)

        def send_hh(h, g):
            nc.sync.dma_start(out=hh_rows[h][R * g : R * (g + 1), :, :], in_=hh[h][g][:])

        for g in range(G):
            softmax_numerators(g)
        weigh(raw[0], 0, 0, gain)
        weigh(raw[1], 0, 1, gain)
        invert(slice(0, 3))
        weigh(raw[2], 0, 2, gain)
        invert(col[3])
        weigh(raw[3], 0, 3, gain)
        normalise_scalar(0)
        normalise_scalar(1)
        normalise_vector(2)
        row_factor(slice(0, 4))
        normalise_vector(3)
        for g in range(G):
            weigh(hh[1][g], 1, g, factor)
        for h in range(2):
            for g in range(G):
                send_hh(h, g)
        quantize(woq)

        y_bank = [bank1, bank2]
        width = [b - a for h, a, b, split in PIECES]
        hq = [operand("hh%d" % k, width[k]) for k in range(len(PIECES))]
        y = [sb.tile([P, G, width[k]], F32, name="y%d" % k) for k in range(len(PIECES))]
        out_v = out.rearrange("g o n -> o g n")

        def interleave_hh(k):
            h, a, b, split = PIECES[k]
            interleave_vector(hq[k][0][:, :split, :], hh_rows[h][:, :, a : a + split])
            dst, src = word_views(hq[k][0][:, split:, :], hh_rows[h][:, :, a + split : b])
            nc.scalar.copy(out=dst, in_=src)

        def second_products(k):
            h, a, b, split = PIECES[k]
            quantize(hq[k])
            for g in range(G):
                product(y_bank[h][g][:, a:b], g, woq, hq[k])

        def finish(k, groups):
            h, a, b, split = PIECES[k]
            cols = slice(HALF * h + a, HALF * h + b)
            for g in range(groups.start, groups.stop):
                nc.vector.tensor_tensor(
                    out=y[k][:, g, :], in0=y_bank[h][g][:, a:b], in1=res_sb[:, g, cols], op=ALU.add,
                )
            nc.sync.dma_start(out=out_v[:, groups, cols], in_=y[k][:, groups, :])

        interleave_hh(0)
        second_products(0)
        interleave_hh(1)
        finish(0, col[0])
        second_products(1)
        for g in range(1, G):
            finish(0, col[g])
        for g in range(G):
            finish(1, col[g])
